import numpy as np
import ml_dtypes


def mxq(x, axis, fmt="e4m3"):
    dtype, down = {"e4m3": (ml_dtypes.float8_e4m3fn, 7), "e5m2": (ml_dtypes.float8_e5m2, 14)}[fmt]
    v = np.moveaxis(np.asarray(x, np.float32).astype(ml_dtypes.bfloat16).astype(np.float64), axis, -1)
    blocks = v.reshape(v.shape[:-1] + (-1, 32))
    amax = np.abs(blocks).max(-1, keepdims=True)
    byte = np.maximum(np.where(amax > 0, np.frexp(amax)[1] - 1 + 127, 0) - down, 1)
    scale = np.exp2(byte - 127.0)
    codes = (blocks / scale).astype(np.float32).astype(dtype).astype(np.float64)
    return np.moveaxis((codes * scale).reshape(v.shape), -1, axis)


WIDE = False


def mx_kscale(k):
    if not WIDE:
        return np.ones(k)
    levels = np.array([10, -10, 5, -5, 0])
    if k % 512:
        return np.exp2(np.random.permutation(np.resize(levels, k // 32))).repeat(32)
    a = np.empty((k // 512, 16))
    for p in range(k // 512):
        a[p, :8] = np.random.permutation(np.resize(levels, 8))
        for g in range(8):
            far = levels[np.abs(levels - a[p, g]) >= 10]
            a[p, g + 8] = far[np.random.randint(len(far))]
    return np.exp2(a.ravel()).repeat(32)


def f64(x):
    return np.asarray(x).astype(np.float64)


def striped(idx):
    return np.tile(idx.reshape(-1, 16).T, (8, 1)).astype(np.uint16)


def unstriped(offs):
    return offs[:16].T.reshape(-1).astype(np.int64)


K, T, E, C, N = 256, 512, 8, 128, 512


def by_expert(wq, xq):
    return np.concatenate([wq[e].T @ xq[:, e * C:(e + 1) * C] for e in range(E)], axis=1)


def setup_inputs():
    n = np.random.standard_normal
    s = mx_kscale(N)[:, None]
    first = np.random.permutation(np.repeat(np.arange(E), T // E))
    second = (first + 1 + np.random.permutation(np.repeat(np.arange(E - 1), -(-T // (E - 1)))[:T])) % E
    while np.bincount(second, minlength=E).max() != T // E:
        load = np.bincount(second, minlength=E); hi, lo = int(load.argmax()), int(load.argmin())
        t = np.flatnonzero((second == hi) & (first != lo))[0]; second[t] = lo
    slot_token = np.empty(E * C, np.int64); pos = np.empty((2, T), np.int64); fill = np.zeros(E, np.int64)
    place = np.stack([np.random.permutation(C) for _ in range(E)])
    for r, deal in enumerate((first, second)):
        for t in np.random.permutation(T):
            e = deal[t]; j = e * C + place[e, fill[e]]; fill[e] += 1; slot_token[j] = t; pos[r, t] = j
    g = np.random.uniform(0.2, 0.8, T)
    w_slot = np.empty(E * C); w_slot[pos[0]] = g; w_slot[pos[1]] = 1.0 - g
    return {
        "dyT": (n((N, T)) * s).astype(np.float32),
        "w": (n((E + 1, N, K)) / np.sqrt(N) / s[None]).astype(np.float32),
        "gate": np.tile(w_slot, (N, 1)).astype(np.float32),
        "offs": striped(slot_token),
        "pos1": striped(pos[0]),
        "pos2": striped(pos[1]),
    }


def reference(dyT, w, gate, offs, pos1, pos2):
    idx = unstriped(offs)
    gq = mxq(f64(gate) * f64(dyT)[:, idx], 0, "e4m3")
    wq = mxq(f64(w), 1, "e4m3")
    ds = wq[E].T @ mxq(f64(dyT), 0, "e4m3")
    dx = by_expert(wq, gq)
    return ds + dx[:, unstriped(pos1)] + dx[:, unstriped(pos2)]

@@ -1,0 +1,155 @@
+from contextlib import ExitStack
+
+import concourse.mybir as mybir
+
+K, T, E, C, N = 256, 512, 8, 128, 512
+S = E * C
+FLOPS = 2 * N * K * (S + T)
+BYTES = 4 * (N * T + (E + 1) * N * K + S + K * T) + 2 * 128 * (S + 2 * T) // 16
+
+F32 = mybir.dt.float32
+BF16 = mybir.dt.bfloat16
+U32 = mybir.dt.uint32
+U16 = mybir.dt.uint16
+U8 = mybir.dt.uint8
+FP8X4 = mybir.dt.float8_e4m3fn_x4
+MULT = mybir.AluOpType.mult
+ADD = mybir.AluOpType.add
+
+P = 128
+PACK = 4
+RUN = 4
+CHUNK = 2 * C
+CHUNKS = S // CHUNK
+KT = K // P
+BANK = 512
+HALF = T // 2
+PER_COL = 16
+
+
+def tile_moe_bds_lin_none_kernel(tc, dyT, w, gate, offs, pos1, pos2, out):
+    nc = tc.nc
+
+    def interleave(engine, dst, src):
+        dst = dst.rearrange("p (c i) j -> p c j i", i=RUN)
+        src = src.rearrange("p j (c i) -> p c j i", i=RUN)
+        if engine == "vector":
+            nc.vector.tensor_copy(out=dst, in_=src)
+        else:
+            nc.scalar.copy(out=dst, in_=src)
+
+    with ExitStack() as ctx:
+        keep = ctx.enter_context(tc.tile_pool(name="keep", bufs=1))
+        psum = ctx.enter_context(tc.psum_pool(name="psum", bufs=1))
+
+        def quantize(name, grouped):
+            width = grouped.shape[1]
+            codes = keep.tile([P, width], U32, name=name + "_codes", align_bytes=64)
+            scales = keep.tile([P, width], U8, name=name + "_scales", align_bytes=64)
+            nc.vector.quantize_mx(
+                out=codes[:].bitcast(FP8X4), scales=scales[:], in_=grouped[:].rearrange("p x j -> p (x j)")
+            )
+            return codes, scales
+
+        def multiply(acc, lhs, lhs_cols, rhs, rhs_cols):
+            nc.tensor.matmul_mx(
+                out=acc,
+                lhsT=lhs[0][:, lhs_cols].bitcast(FP8X4),
+                lhsT_scale=lhs[1][:, lhs_cols],
+                rhs=rhs[0][:, rhs_cols].bitcast(FP8X4),
+                rhs_scale=rhs[1][:, rhs_cols],
+                start=True,
+                stop=True,
+            )
+
+        offs_sb = keep.tile([P, S // PER_COL], U16, name="offs_sb")
+        pos1_sb = keep.tile([P, T // PER_COL], U16, name="pos1_sb")
+        pos2_sb = keep.tile([P, T // PER_COL], U16, name="pos2_sb")
+        gate_sb = keep.tile([P, S], F32, name="gate_sb")
+        dy_rows = dyT.rearrange("(p j) t -> p j t", j=PACK)
+        dy_plane = [keep.tile([P, T], F32, name="dy_plane%d" % j) for j in range(PACK)]
+        dy_all = keep.tile([P, PACK, T], F32, name="dy_all")
+        w_raw = [keep.tile([P, PACK, K], F32, name="w_raw%d" % e) for e in range(E + 1)]
+
+        def load_gate(lo, hi):
+            nc.sync.dma_start(out=gate_sb[:, lo:hi], in_=gate[0:P, lo:hi])
+
+        def load_w(e):
+            nc.sync.dma_start(out=w_raw[e][:], in_=w[e].rearrange("(p j) k -> p j k", j=PACK))
+
+        nc.sync.dma_start(offs_sb[:], offs)
+        load_gate(0, CHUNK)
+        for j in range(PACK):
+            nc.sync.dma_start(out=dy_plane[j][:], in_=dy_rows[:, j, :])
+        load_gate(CHUNK, 2 * CHUNK)
+        load_w(0)
+        load_w(1)
+        load_gate(2 * CHUNK, S)
+        for e in range(2, E):
+            load_w(e)
+        nc.sync.dma_start(pos1_sb[:], pos1)
+        nc.sync.dma_start(pos2_sb[:], pos2)
+        nc.sync.dma_start(out=dy_all[:], in_=dy_rows)
+        load_w(E)
+
+        dx_ps = [[psum.tile([P, BANK], F32, name="dx_ps%d_%d" % (kt, b)) for b in range(S // BANK)] for kt in range(KT)]
+        ds_ps = [psum.tile([P, T], F32, name="ds_ps%d" % kt) for kt in range(KT)]
+        dx_sb = [keep.tile([P, S], F32, name="dx_sb%d" % kt) for kt in range(KT)]
+
+        g_mx = []
+
+        def make_g(c, engine):
+            slots = slice(c * CHUNK, (c + 1) * CHUNK)
+            entries = offs_sb[:, slots.start // PER_COL : slots.stop // PER_COL]
+            g_raw = keep.tile([P, PACK, CHUNK], F32, name="g_raw%d" % c)
+            for j in range(PACK):
+                nc.vector.tensor_tensor(g_raw[:, j, :], dy_plane[j][:].indirect(entries), gate_sb[:, slots], MULT)
+            grouped = keep.tile([P, CHUNK, PACK], BF16, name="g_grouped%d" % c, align_bytes=64)
+            interleave(engine, grouped[:], g_raw[:])
+            g_mx.append(quantize("g%d" % c, grouped))
+
+        def routed(c, kt, engine):
+            name = "w%d_%d" % (c, kt)
+            grouped = keep.tile([P, 2 * P, PACK], BF16, name=name + "_grouped", align_bytes=64)
+            for i in range(2):
+                interleave(engine, grouped[:, i * P : (i + 1) * P, :], w_raw[2 * c + i][:, :, kt * P : (kt + 1) * P])
+            w_mx = quantize(name, grouped)
+            for i in range(2):
+                b, col = divmod((2 * c + i) * C, BANK)
+                multiply(dx_ps[kt][b][:, col : col + C], w_mx, slice(i * P, (i + 1) * P), g_mx[c], slice(i * C, (i + 1) * C))
+            if (c + 1) * CHUNK % BANK == 0:
+                b = c * CHUNK // BANK
+                nc.scalar.copy(out=dx_sb[kt][:, b * BANK : (b + 1) * BANK], in_=dx_ps[kt][b][:])
+
+        for c in range(CHUNKS):
+            make_g(c, "vector" if c == CHUNKS - 1 else "scalar")
+            routed(c, 0, "scalar")
+        for c in range(CHUNKS):
+            routed(c, 1, "scalar" if c < 2 else "vector")
+
+        ws_grouped = keep.tile([P, K, PACK], BF16, name="ws_grouped", align_bytes=64)
+        interleave("scalar", ws_grouped[:], w_raw[E][:])
+        ws_mx = quantize("ws", ws_grouped)
+        dy_grouped = keep.tile([P, T, PACK], BF16, name="dy_grouped", align_bytes=64)
+        interleave("scalar", dy_grouped[:], dy_all[:])
+        dy_mx = quantize("dy", dy_grouped)
+        for kt in range(KT):
+            multiply(ds_ps[kt][:], ws_mx, slice(kt * P, (kt + 1) * P), dy_mx, slice(0, T))
+
+        for kt in range(KT):
+            first = keep.tile([P, T], F32, name="first%d" % kt)
+            second = keep.tile([P, T], F32, name="second%d" % kt)
+            pair = keep.tile([P, T], F32, name="pair%d" % kt)
+            total = keep.tile([P, T], F32, name="total%d" % kt)
+            for h in range(2):
+                tokens = slice(h * HALF, (h + 1) * HALF)
+                entries = slice(tokens.start // PER_COL, tokens.stop // PER_COL)
+                nc.vector.tensor_copy(first[:, tokens], dx_sb[kt][:].indirect(pos1_sb[:, entries]))
+                nc.vector.tensor_copy(second[:, tokens], dx_sb[kt][:].indirect(pos2_sb[:, entries]))
+            for h in range(2):
+                tokens = slice(h * HALF, (h + 1) * HALF)
+                nc.vector.tensor_tensor(pair[:, tokens], first[:, tokens], second[:, tokens], ADD)
+            for h in range(2):
+                tokens = slice(h * HALF, (h + 1) * HALF)
+                nc.vector.tensor_tensor(total[:, tokens], pair[:, tokens], ds_ps[kt][:, tokens], ADD)
+                nc.sync.dma_start(out=out[kt * P : (kt + 1) * P, tokens], in_=total[:, tokens])

@@ -19,35 +19,36 @@ ADD = mybir.AluOpType.add
 P = 128
 PACK = 4
 RUN = 4
-CHUNK = 2 * C
-CHUNKS = S // CHUNK
-KT = K // P
-BANK = 512
-HALF = T // 2
 PER_COL = 16
+BANK = 512
+CHUNK = 2 * C
+HALF = T // 2
+WIDE = S - CHUNK + 32
+LAST = PACK - 1
 
 
 def tile_moe_bds_lin_none_kernel(tc, dyT, w, gate, offs, pos1, pos2, out):
     nc = tc.nc
 
-    def interleave(engine, dst, src):
-        dst = dst.rearrange("p (c i) j -> p c j i", i=RUN)
-        src = src.rearrange("p j (c i) -> p c j i", i=RUN)
-        if engine == "vector":
-            nc.vector.tensor_copy(out=dst, in_=src)
-        else:
-            nc.scalar.copy(out=dst, in_=src)
-
     with ExitStack() as ctx:
         keep = ctx.enter_context(tc.tile_pool(name="keep", bufs=1))
         psum = ctx.enter_context(tc.psum_pool(name="psum", bufs=1))
 
-        def quantize(name, grouped):
-            width = grouped.shape[1]
+        def entries(tile, cols):
+            return tile[:, cols.start // PER_COL : cols.stop // PER_COL]
+
+        def quantize(name, copy, sources):
+            width = sum(src.shape[2] for src in sources)
+            grouped = keep.tile([P, width, PACK], BF16, name=name + "_grouped", align_bytes=64)
             codes = keep.tile([P, width], U32, name=name + "_codes", align_bytes=64)
             scales = keep.tile([P, width], U8, name=name + "_scales", align_bytes=64)
+            col = 0
+            for src in sources:
+                dst = grouped[:, col : col + src.shape[2], :]
+                copy(out=dst.rearrange("p (c i) r -> p c r i", i=RUN), in_=src.rearrange("p r (c i) -> p c r i", i=RUN))
+                col += src.shape[2]
             nc.vector.quantize_mx(
-                out=codes[:].bitcast(FP8X4), scales=scales[:], in_=grouped[:].rearrange("p x j -> p (x j)")
+                out=codes[:].bitcast(FP8X4), scales=scales[:], in_=grouped[:].rearrange("p x r -> p (x r)")
             )
             return codes, scales
 
@@ -62,94 +63,131 @@ def tile_moe_bds_lin_none_kernel(tc, dyT, w, gate, offs, pos1, pos2, out):
                 stop=True,
             )
 
+        on_scalar, on_vector = nc.scalar.copy, nc.vector.tensor_copy
+        chunk = [slice(c * CHUNK, (c + 1) * CHUNK) for c in range(S // CHUNK)]
+        half = [slice(0, HALF), slice(HALF, T)]
+        k_tile = [slice(0, P), slice(P, K)]
+        later = slice(CHUNK, S)
+
+        window = [keep.tile([P, T if r == LAST else WIDE], F32, name="window%d" % r) for r in range(PACK)]
+        for r in range(LAST):
+            nc.vector.memset(window[r][:, T:], 0.0)
+
         offs_sb = keep.tile([P, S // PER_COL], U16, name="offs_sb")
         pos1_sb = keep.tile([P, T // PER_COL], U16, name="pos1_sb")
         pos2_sb = keep.tile([P, T // PER_COL], U16, name="pos2_sb")
         gate_sb = keep.tile([P, S], F32, name="gate_sb")
-        dy_rows = dyT.rearrange("(p j) t -> p j t", j=PACK)
-        dy_plane = [keep.tile([P, T], F32, name="dy_plane%d" % j) for j in range(PACK)]
-        dy_all = keep.tile([P, PACK, T], F32, name="dy_all")
         w_raw = [keep.tile([P, PACK, K], F32, name="w_raw%d" % e) for e in range(E + 1)]
+        dy_raw = [keep.tile([P, PACK, HALF], F32, name="dy_raw%d" % h) for h in range(2)]
+        dy_rows = dyT.rearrange("(p r) t -> p r t", r=PACK)
 
-        def load_gate(lo, hi):
-            nc.sync.dma_start(out=gate_sb[:, lo:hi], in_=gate[0:P, lo:hi])
-
-        def load_w(e):
-            nc.sync.dma_start(out=w_raw[e][:], in_=w[e].rearrange("(p j) k -> p j k", j=PACK))
+        def load_w(experts):
+            for e in experts:
+                nc.sync.dma_start(out=w_raw[e][:], in_=w[e].rearrange("(p r) k -> p r k", r=PACK))
 
         nc.sync.dma_start(offs_sb[:], offs)
-        load_gate(0, CHUNK)
-        for j in range(PACK):
-            nc.sync.dma_start(out=dy_plane[j][:], in_=dy_rows[:, j, :])
-        load_gate(CHUNK, 2 * CHUNK)
-        load_w(0)
-        load_w(1)
-        load_gate(2 * CHUNK, S)
-        for e in range(2, E):
-            load_w(e)
+        nc.sync.dma_start(out=gate_sb[:, chunk[0]], in_=gate[0:P, chunk[0]])
+        for r in range(LAST):
+            nc.sync.dma_start(out=window[r][:, 0:T], in_=dy_rows[:, r, :])
+        nc.sync.dma_start(out=gate_sb[:, later], in_=gate[0:P, later])
+        load_w([0, 2, 5])
         nc.sync.dma_start(pos1_sb[:], pos1)
+        load_w([1])
+        nc.sync.dma_start(out=window[LAST][:], in_=dy_rows[:, LAST, :])
+        load_w([4, 6, 7, 3])
         nc.sync.dma_start(pos2_sb[:], pos2)
-        nc.sync.dma_start(out=dy_all[:], in_=dy_rows)
-        load_w(E)
+        load_w([E])
+        for h in range(2):
+            nc.sync.dma_start(out=dy_raw[h][:], in_=dy_rows[:, :, half[h]])
 
-        dx_ps = [[psum.tile([P, BANK], F32, name="dx_ps%d_%d" % (kt, b)) for b in range(S // BANK)] for kt in range(KT)]
-        ds_ps = [psum.tile([P, T], F32, name="ds_ps%d" % kt) for kt in range(KT)]
-        dx_sb = [keep.tile([P, S], F32, name="dx_sb%d" % kt) for kt in range(KT)]
+        g_first = keep.tile([P, PACK, CHUNK], F32, name="g_first")
+        g_later = keep.tile([P, PACK, S - CHUNK], F32, name="g_later")
+        g_raw = [g_first[:]] + [g_later[:, :, chunk[c]] for c in range(len(chunk) - 1)]
 
-        g_mx = []
+        def gather_g(dst, r, slots):
+            nc.vector.tensor_tensor(dst, window[r][:].indirect(entries(offs_sb, slots)), gate_sb[:, slots], MULT)
 
-        def make_g(c, engine):
-            slots = slice(c * CHUNK, (c + 1) * CHUNK)
-            entries = offs_sb[:, slots.start // PER_COL : slots.stop // PER_COL]
-            g_raw = keep.tile([P, PACK, CHUNK], F32, name="g_raw%d" % c)
-            for j in range(PACK):
-                nc.vector.tensor_tensor(g_raw[:, j, :], dy_plane[j][:].indirect(entries), gate_sb[:, slots], MULT)
-            grouped = keep.tile([P, CHUNK, PACK], BF16, name="g_grouped%d" % c, align_bytes=64)
-            interleave(engine, grouped[:], g_raw[:])
-            g_mx.append(quantize("g%d" % c, grouped))
+        for r in range(PACK):
+            gather_g(g_first[:, r, :], r, chunk[0])
+        for r in range(LAST):
+            gather_g(g_later[:, r, :], r, later)
+        for c in (3, 1, 2):
+            gather_g(g_raw[c][:, LAST, :], LAST, chunk[c])
 
-        def routed(c, kt, engine):
-            name = "w%d_%d" % (c, kt)
-            grouped = keep.tile([P, 2 * P, PACK], BF16, name=name + "_grouped", align_bytes=64)
-            for i in range(2):
-                interleave(engine, grouped[:, i * P : (i + 1) * P, :], w_raw[2 * c + i][:, :, kt * P : (kt + 1) * P])
-            w_mx = quantize(name, grouped)
-            for i in range(2):
-                b, col = divmod((2 * c + i) * C, BANK)
-                multiply(dx_ps[kt][b][:, col : col + C], w_mx, slice(i * P, (i + 1) * P), g_mx[c], slice(i * C, (i + 1) * C))
-            if (c + 1) * CHUNK % BANK == 0:
-                b = c * CHUNK // BANK
-                nc.scalar.copy(out=dx_sb[kt][:, b * BANK : (b + 1) * BANK], in_=dx_ps[kt][b][:])
+        g_mx, w_mx, dy_mx = {}, {}, {}
 
-        for c in range(CHUNKS):
-            make_g(c, "vector" if c == CHUNKS - 1 else "scalar")
-            routed(c, 0, "scalar")
-        for c in range(CHUNKS):
-            routed(c, 1, "scalar" if c < 2 else "vector")
+        def quantize_g(c, copy):
+            g_mx[c] = quantize("g%d" % c, copy, [g_raw[c]])
 
-        ws_grouped = keep.tile([P, K, PACK], BF16, name="ws_grouped", align_bytes=64)
-        interleave("scalar", ws_grouped[:], w_raw[E][:])
-        ws_mx = quantize("ws", ws_grouped)
-        dy_grouped = keep.tile([P, T, PACK], BF16, name="dy_grouped", align_bytes=64)
-        interleave("scalar", dy_grouped[:], dy_all[:])
-        dy_mx = quantize("dy", dy_grouped)
-        for kt in range(KT):
-            multiply(ds_ps[kt][:], ws_mx, slice(kt * P, (kt + 1) * P), dy_mx, slice(0, T))
+        def quantize_w(kt, c, copy):
+            w_mx[kt, c] = quantize("w%d_%d" % (kt, c), copy, [w_raw[2 * c + i][:, :, k_tile[kt]] for i in range(2)])
 
-        for kt in range(KT):
-            first = keep.tile([P, T], F32, name="first%d" % kt)
-            second = keep.tile([P, T], F32, name="second%d" % kt)
-            pair = keep.tile([P, T], F32, name="pair%d" % kt)
-            total = keep.tile([P, T], F32, name="total%d" % kt)
-            for h in range(2):
-                tokens = slice(h * HALF, (h + 1) * HALF)
-                entries = slice(tokens.start // PER_COL, tokens.stop // PER_COL)
-                nc.vector.tensor_copy(first[:, tokens], dx_sb[kt][:].indirect(pos1_sb[:, entries]))
-                nc.vector.tensor_copy(second[:, tokens], dx_sb[kt][:].indirect(pos2_sb[:, entries]))
-            for h in range(2):
-                tokens = slice(h * HALF, (h + 1) * HALF)
-                nc.vector.tensor_tensor(pair[:, tokens], first[:, tokens], second[:, tokens], ADD)
-            for h in range(2):
-                tokens = slice(h * HALF, (h + 1) * HALF)
-                nc.vector.tensor_tensor(total[:, tokens], pair[:, tokens], ds_ps[kt][:, tokens], ADD)
-                nc.sync.dma_start(out=out[kt * P : (kt + 1) * P, tokens], in_=total[:, tokens])
+        def quantize_dy(h):
+            dy_mx[h] = quantize("dy%d" % h, on_scalar, [dy_raw[h][:]])
+
+        dx_ps = [[psum.tile([P, BANK], F32, name="dx_ps%d_%d" % (kt, b)) for b in range(S // BANK)] for kt in range(2)]
+        dx_sb = [keep.tile([P, S], F32, name="dx_sb%d" % kt) for kt in range(2)]
+
+        def multiply_experts(kt):
+            for e in range(E):
+                c, i = divmod(e, 2)
+                b, col = divmod(e * C, BANK)
+                cols = slice(i * C, (i + 1) * C)
+                multiply(dx_ps[kt][b][:, col : col + C], w_mx[kt, c], cols, g_mx[c], cols)
+
+        def copy_dx(kt, b):
+            nc.scalar.copy(out=dx_sb[kt][:, b * BANK : (b + 1) * BANK], in_=dx_ps[kt][b][:])
+
+        quantize_g(0, on_scalar)
+        quantize_g(3, on_scalar)
+        quantize_dy(0)
+        quantize_w(0, 0, on_scalar)
+        quantize_g(2, on_vector)
+        for c in range(1, len(chunk)):
+            quantize_w(0, c, on_scalar)
+        quantize_g(1, on_scalar)
+        multiply_experts(0)
+        for c in range(len(chunk) - 1):
+            quantize_w(1, c, on_scalar)
+        copy_dx(0, 1)
+        copy_dx(0, 0)
+        quantize_w(1, 3, on_vector)
+        multiply_experts(1)
+        copy_dx(1, 0)
+        copy_dx(1, 1)
+
+        quantize_dy(1)
+        shared_mx = quantize("shared", on_vector, [w_raw[E][:]])
+        ds_ps = [[psum.tile([P, BANK], F32, name="ds_ps%d_%d" % (kt, h)) for h in range(2)] for kt in range(2)]
+        for h in range(2):
+            for kt in range(2):
+                multiply(ds_ps[kt][h][:, 0:HALF], shared_mx, k_tile[kt], dy_mx[h], slice(0, HALF))
+
+        late = keep.tile([P, 3, HALF], F32, name="late", tag="dy1_grouped", align_bytes=64)
+        first = [keep.tile([P, T], F32, name="first%d" % kt) for kt in range(2)]
+        second0 = keep.tile([P, T], F32, name="second0")
+        second1_low = keep.tile([P, HALF], F32, name="second1_low")
+        second1 = [second1_low[:], late[:, 0, :]]
+        both = [keep.tile([P, T], F32, name="both%d" % kt) for kt in range(2)]
+        total_high = [keep.tile([P, HALF], F32, name="total_high%d" % kt) for kt in range(2)]
+        total = [[late[:, 1 + kt, :], total_high[kt][:]] for kt in range(2)]
+
+        def gather_dx(dst, kt, pos_sb, tokens):
+            nc.vector.tensor_copy(dst, dx_sb[kt][:].indirect(entries(pos_sb, tokens)))
+
+        def finish(kt, h):
+            nc.vector.tensor_tensor(total[kt][h], both[kt][:, half[h]], ds_ps[kt][h][:, 0:HALF], ADD)
+            nc.sync.dma_start(out=out[k_tile[kt], half[h]], in_=total[kt][h])
+
+        gather_dx(first[0][:], 0, pos1_sb, slice(0, T))
+        gather_dx(second0[:], 0, pos2_sb, slice(0, T))
+        nc.gpsimd.tensor_tensor(both[0][:], first[0][:], second0[:], ADD)
+        finish(0, 1)
+        gather_dx(first[1][:], 1, pos1_sb, slice(0, T))
+        for h in range(2):
+            gather_dx(second1[h], 1, pos2_sb, half[h])
+        finish(0, 0)
+        nc.gpsimd.tensor_tensor(both[1][:, half[0]], first[1][:, half[0]], second1[0], ADD)
+        nc.vector.tensor_tensor(both[1][:, half[1]], first[1][:, half[1]], second1[1], ADD)
+        finish(1, 0)
+        finish(1, 1)

from contextlib import ExitStack

import concourse.mybir as mybir

K, T, E, C, N = 256, 512, 8, 128, 512
S = E * C
FLOPS = 2 * N * K * (S + T)
BYTES = 4 * (N * T + (E + 1) * N * K + S + K * T) + 2 * 128 * (S + 2 * T) // 16

F32 = mybir.dt.float32
BF16 = mybir.dt.bfloat16
U32 = mybir.dt.uint32
U16 = mybir.dt.uint16
U8 = mybir.dt.uint8
FP8X4 = mybir.dt.float8_e4m3fn_x4
MULT = mybir.AluOpType.mult
ADD = mybir.AluOpType.add

P = 128
PACK = 4
RUN = 4
PER_COL = 16
BANK = 512
CHUNK = 2 * C
HALF = T // 2
WIDE = S - CHUNK + 32
LAST = PACK - 1


def tile_moe_bds_lin_none_kernel(tc, dyT, w, gate, offs, pos1, pos2, out):
    nc = tc.nc

    with ExitStack() as ctx:
        keep = ctx.enter_context(tc.tile_pool(name="keep", bufs=1))
        psum = ctx.enter_context(tc.psum_pool(name="psum", bufs=1))

        def entries(tile, cols):
            return tile[:, cols.start // PER_COL : cols.stop // PER_COL]

        def quantize(name, copy, sources):
            width = sum(src.shape[2] for src in sources)
            grouped = keep.tile([P, width, PACK], BF16, name=name + "_grouped", align_bytes=64)
            codes = keep.tile([P, width], U32, name=name + "_codes", align_bytes=64)
            scales = keep.tile([P, width], U8, name=name + "_scales", align_bytes=64)
            col = 0
            for src in sources:
                dst = grouped[:, col : col + src.shape[2], :]
                copy(out=dst.rearrange("p (c i) r -> p c r i", i=RUN), in_=src.rearrange("p r (c i) -> p c r i", i=RUN))
                col += src.shape[2]
            nc.vector.quantize_mx(
                out=codes[:].bitcast(FP8X4), scales=scales[:], in_=grouped[:].rearrange("p x r -> p (x r)")
            )
            return codes, scales

        def multiply(acc, lhs, lhs_cols, rhs, rhs_cols):
            nc.tensor.matmul_mx(
                out=acc,
                lhsT=lhs[0][:, lhs_cols].bitcast(FP8X4),
                lhsT_scale=lhs[1][:, lhs_cols],
                rhs=rhs[0][:, rhs_cols].bitcast(FP8X4),
                rhs_scale=rhs[1][:, rhs_cols],
                start=True,
                stop=True,
            )

        on_scalar, on_vector = nc.scalar.copy, nc.vector.tensor_copy
        chunk = [slice(c * CHUNK, (c + 1) * CHUNK) for c in range(S // CHUNK)]
        half = [slice(0, HALF), slice(HALF, T)]
        k_tile = [slice(0, P), slice(P, K)]
        later = slice(CHUNK, S)

        window = [keep.tile([P, T if r == LAST else WIDE], F32, name="window%d" % r) for r in range(PACK)]
        for r in range(LAST):
            nc.vector.memset(window[r][:, T:], 0.0)

        offs_sb = keep.tile([P, S // PER_COL], U16, name="offs_sb")
        pos1_sb = keep.tile([P, T // PER_COL], U16, name="pos1_sb")
        pos2_sb = keep.tile([P, T // PER_COL], U16, name="pos2_sb")
        gate_sb = keep.tile([P, S], F32, name="gate_sb")
        w_raw = [keep.tile([P, PACK, K], F32, name="w_raw%d" % e) for e in range(E + 1)]
        dy_raw = [keep.tile([P, PACK, HALF], F32, name="dy_raw%d" % h) for h in range(2)]
        dy_rows = dyT.rearrange("(p r) t -> p r t", r=PACK)

        def load_w(experts):
            for e in experts:
                nc.sync.dma_start(out=w_raw[e][:], in_=w[e].rearrange("(p r) k -> p r k", r=PACK))

        nc.sync.dma_start(offs_sb[:], offs)
        nc.sync.dma_start(out=gate_sb[:, chunk[0]], in_=gate[0:P, chunk[0]])
        for r in range(LAST):
            nc.sync.dma_start(out=window[r][:, 0:T], in_=dy_rows[:, r, :])
        nc.sync.dma_start(out=gate_sb[:, later], in_=gate[0:P, later])
        load_w([0, 2, 5])
        nc.sync.dma_start(pos1_sb[:], pos1)
        load_w([1])
        nc.sync.dma_start(out=window[LAST][:], in_=dy_rows[:, LAST, :])
        load_w([4, 6, 7, 3])
        nc.sync.dma_start(pos2_sb[:], pos2)
        load_w([E])
        for h in range(2):
            nc.sync.dma_start(out=dy_raw[h][:], in_=dy_rows[:, :, half[h]])

        g_first = keep.tile([P, PACK, CHUNK], F32, name="g_first")
        g_later = keep.tile([P, PACK, S - CHUNK], F32, name="g_later")
        g_raw = [g_first[:]] + [g_later[:, :, chunk[c]] for c in range(len(chunk) - 1)]

        def gather_g(dst, r, slots):
            nc.vector.tensor_tensor(dst, window[r][:].indirect(entries(offs_sb, slots)), gate_sb[:, slots], MULT)

        for r in range(PACK):
            gather_g(g_first[:, r, :], r, chunk[0])
        for r in range(LAST):
            gather_g(g_later[:, r, :], r, later)
        for c in (3, 1, 2):
            gather_g(g_raw[c][:, LAST, :], LAST, chunk[c])

        g_mx, w_mx, dy_mx = {}, {}, {}

        def quantize_g(c, copy):
            g_mx[c] = quantize("g%d" % c, copy, [g_raw[c]])

        def quantize_w(kt, c, copy):
            w_mx[kt, c] = quantize("w%d_%d" % (kt, c), copy, [w_raw[2 * c + i][:, :, k_tile[kt]] for i in range(2)])

        def quantize_dy(h):
            dy_mx[h] = quantize("dy%d" % h, on_scalar, [dy_raw[h][:]])

        dx_ps = [[psum.tile([P, BANK], F32, name="dx_ps%d_%d" % (kt, b)) for b in range(S // BANK)] for kt in range(2)]
        dx_sb = [keep.tile([P, S], F32, name="dx_sb%d" % kt) for kt in range(2)]

        def multiply_experts(kt):
            for e in range(E):
                c, i = divmod(e, 2)
                b, col = divmod(e * C, BANK)
                cols = slice(i * C, (i + 1) * C)
                multiply(dx_ps[kt][b][:, col : col + C], w_mx[kt, c], cols, g_mx[c], cols)

        def copy_dx(kt, b):
            nc.scalar.copy(out=dx_sb[kt][:, b * BANK : (b + 1) * BANK], in_=dx_ps[kt][b][:])

        quantize_g(0, on_scalar)
        quantize_g(3, on_scalar)
        quantize_dy(0)
        quantize_w(0, 0, on_scalar)
        quantize_g(2, on_vector)
        for c in range(1, len(chunk)):
            quantize_w(0, c, on_scalar)
        quantize_g(1, on_scalar)
        multiply_experts(0)
        for c in range(len(chunk) - 1):
            quantize_w(1, c, on_scalar)
        copy_dx(0, 1)
        copy_dx(0, 0)
        quantize_w(1, 3, on_vector)
        multiply_experts(1)
        copy_dx(1, 0)
        copy_dx(1, 1)

        quantize_dy(1)
        shared_mx = quantize("shared", on_vector, [w_raw[E][:]])
        ds_ps = [[psum.tile([P, BANK], F32, name="ds_ps%d_%d" % (kt, h)) for h in range(2)] for kt in range(2)]
        for h in range(2):
            for kt in range(2):
                multiply(ds_ps[kt][h][:, 0:HALF], shared_mx, k_tile[kt], dy_mx[h], slice(0, HALF))

        late = keep.tile([P, 3, HALF], F32, name="late", tag="dy1_grouped", align_bytes=64)
        first = [keep.tile([P, T], F32, name="first%d" % kt) for kt in range(2)]
        second0 = keep.tile([P, T], F32, name="second0")
        second1_low = keep.tile([P, HALF], F32, name="second1_low")
        second1 = [second1_low[:], late[:, 0, :]]
        both = [keep.tile([P, T], F32, name="both%d" % kt) for kt in range(2)]
        total_high = [keep.tile([P, HALF], F32, name="total_high%d" % kt) for kt in range(2)]
        total = [[late[:, 1 + kt, :], total_high[kt][:]] for kt in range(2)]

        def gather_dx(dst, kt, pos_sb, tokens):
            nc.vector.tensor_copy(dst, dx_sb[kt][:].indirect(entries(pos_sb, tokens)))

        def finish(kt, h):
            nc.vector.tensor_tensor(total[kt][h], both[kt][:, half[h]], ds_ps[kt][h][:, 0:HALF], ADD)
            nc.sync.dma_start(out=out[k_tile[kt], half[h]], in_=total[kt][h])

        gather_dx(first[0][:], 0, pos1_sb, slice(0, T))
        gather_dx(second0[:], 0, pos2_sb, slice(0, T))
        nc.gpsimd.tensor_tensor(both[0][:], first[0][:], second0[:], ADD)
        finish(0, 1)
        gather_dx(first[1][:], 1, pos1_sb, slice(0, T))
        for h in range(2):
            gather_dx(second1[h], 1, pos2_sb, half[h])
        finish(0, 0)
        nc.gpsimd.tensor_tensor(both[1][:, half[0]], first[1][:, half[0]], second1[0], ADD)
        nc.vector.tensor_tensor(both[1][:, half[1]], first[1][:, half[1]], second1[1], ADD)
        finish(1, 0)
        finish(1, 1)
